import numpy as np
import ml_dtypes

BF16 = ml_dtypes.bfloat16


def bf(x):
    return np.asarray(x, np.float32).astype(BF16)


def f32(x):
    return np.asarray(x, np.float32)


def f64(x):
    return np.asarray(x).astype(np.float64)


def striped(idx):
    return np.tile(idx.reshape(-1, 16).T, (8, 1))


S, K, M, N, V, F = 1024, 128, 128, 2304, 384, 6


def gelu_tanh(v):
    return 0.5 * v * (1.0 + np.tanh(np.sqrt(2.0 / np.pi) * (v + 0.044715 * v**3)))


def setup_inputs():
    return {"table": bf(np.random.standard_normal((F, K, S))), "w": bf(np.random.standard_normal((K, M)) / np.sqrt(F * K)), "b": f32(0.5 * np.random.standard_normal((M, 1))), "offs": striped(np.concatenate([np.random.permutation(np.tile(np.arange(S), 2))[:V] for _ in range(F)]))}


def reference(table, w, b, offs):
    idx = offs[:16].T.reshape(-1)
    y = f64(w).T @ sum(f64(table)[f][:, idx[f * V : (f + 1) * V]] for f in range(F))
    return gelu_tanh(y + f64(b))

@@ -1,0 +1,37 @@
+import concourse.mybir as mybir
+
+F32, BF16, U16 = mybir.dt.float32, mybir.dt.bfloat16, mybir.dt.uint16
+GELU = mybir.ActivationFunctionType.Gelu_apprx_tanh
+ENTRIES_PER_COLUMN = 16
+
+FLOPS = 2 * 128 * 128 * 2304
+
+
+def tile_rows_fields_gelu_rep_kernel(tc, table, w, b, offs, out):
+    nc = tc.nc
+    codebooks, features, codes = table.shape
+    channels, frames = out.shape
+    list_columns = frames // ENTRIES_PER_COLUMN
+
+    with (
+        tc.tile_pool(name="held", bufs=1) as held,
+        tc.psum_pool(name="psum", bufs=1) as psum,
+    ):
+        offsets = held.tile(list(offs.shape), U16, name="offsets")
+        weights = held.tile([features, channels], BF16, name="weights")
+        bias = held.tile([channels, 1], F32, name="bias")
+        books = [held.tile([features, codes], BF16, name=f"book{f}") for f in range(codebooks)]
+        nc.sync.dma_start(offsets[:], offs)
+        nc.sync.dma_start(weights[:], w)
+        for f in range(codebooks):
+            nc.sync.dma_start(books[f][:], table[f])
+        nc.scalar.dma_start(bias[:], b)
+
+        total = psum.tile([channels, frames], F32, name="total")
+        for f in range(codebooks):
+            picked = books[f][:].indirect(offsets[:, f * list_columns : (f + 1) * list_columns])
+            nc.tensor.matmul(total[:], weights[:], picked, start=(f == 0), stop=(f == codebooks - 1))
+
+        result = held.tile([channels, frames], F32, name="result")
+        nc.scalar.activation(result[:], total[:], GELU, bias=bias[:])
+        nc.sync.dma_start(out, result[:])

@@ -20,16 +20,24 @@ def tile_rows_fields_gelu_rep_kernel(tc, table, w, b, offs, out):
         offsets = held.tile(list(offs.shape), U16, name="offsets")
         weights = held.tile([features, channels], BF16, name="weights")
         bias = held.tile([channels, 1], F32, name="bias")
-        books = [held.tile([features, codes], BF16, name=f"book{f}") for f in range(codebooks)]
-        nc.sync.dma_start(offsets[:], offs)
-        nc.sync.dma_start(weights[:], w)
-        for f in range(codebooks):
-            nc.sync.dma_start(books[f][:], table[f])
+
+        windows = []
+        for first in range(0, codebooks - 2, 2):
+            pair = held.tile([features, 2, codes], BF16, name=f"pair{first}")
+            nc.sync.dma_start(pair[:], table[first : first + 2].rearrange("f k s -> k f s"))
+            windows.extend([pair[:, 0, :], pair[:, 1, :]])
+            if first == 0:
+                nc.sync.dma_start(offsets[:], offs)
+        for f in range(codebooks - 2, codebooks):
+            single = held.tile([features, codes], BF16, name=f"single{f}")
+            nc.sync.dma_start(single[:], table[f])
+            windows.append(single[:])
+        nc.scalar.dma_start(weights[:], w)
         nc.scalar.dma_start(bias[:], b)
 
         total = psum.tile([channels, frames], F32, name="total")
         for f in range(codebooks):
-            picked = books[f][:].indirect(offsets[:, f * list_columns : (f + 1) * list_columns])
+            picked = windows[f].indirect(offsets[:, f * list_columns : (f + 1) * list_columns])
             nc.tensor.matmul(total[:], weights[:], picked, start=(f == 0), stop=(f == codebooks - 1))
 
         result = held.tile([channels, frames], F32, name="result")

@@ -21,19 +21,19 @@ def tile_rows_fields_gelu_rep_kernel(tc, table, w, b, offs, out):
         weights = held.tile([features, channels], BF16, name="weights")
         bias = held.tile([channels, 1], F32, name="bias")
 
+        nc.sync.dma_start(offsets[:], offs)
+        nc.sync.dma_start(weights[:], w)
+        nc.sync.dma_start(bias[:], b)
+
         windows = []
         for first in range(0, codebooks - 2, 2):
             pair = held.tile([features, 2, codes], BF16, name=f"pair{first}")
-            nc.sync.dma_start(pair[:], table[first : first + 2].rearrange("f k s -> k f s"))
+            nc.scalar.dma_start(pair[:], table[first : first + 2].rearrange("f k s -> k f s"))
             windows.extend([pair[:, 0, :], pair[:, 1, :]])
-            if first == 0:
-                nc.sync.dma_start(offsets[:], offs)
         for f in range(codebooks - 2, codebooks):
             single = held.tile([features, codes], BF16, name=f"single{f}")
-            nc.sync.dma_start(single[:], table[f])
+            nc.scalar.dma_start(single[:], table[f])
             windows.append(single[:])
-        nc.scalar.dma_start(weights[:], w)
-        nc.scalar.dma_start(bias[:], b)
 
         total = psum.tile([channels, frames], F32, name="total")
         for f in range(codebooks):

import concourse.mybir as mybir

F32, BF16, U16 = mybir.dt.float32, mybir.dt.bfloat16, mybir.dt.uint16
GELU = mybir.ActivationFunctionType.Gelu_apprx_tanh
ENTRIES_PER_COLUMN = 16

FLOPS = 2 * 128 * 128 * 2304


def tile_rows_fields_gelu_rep_kernel(tc, table, w, b, offs, out):
    nc = tc.nc
    codebooks, features, codes = table.shape
    channels, frames = out.shape
    list_columns = frames // ENTRIES_PER_COLUMN

    with (
        tc.tile_pool(name="held", bufs=1) as held,
        tc.psum_pool(name="psum", bufs=1) as psum,
    ):
        offsets = held.tile(list(offs.shape), U16, name="offsets")
        weights = held.tile([features, channels], BF16, name="weights")
        bias = held.tile([channels, 1], F32, name="bias")

        nc.sync.dma_start(offsets[:], offs)
        nc.sync.dma_start(weights[:], w)
        nc.sync.dma_start(bias[:], b)

        windows = []
        for first in range(0, codebooks - 2, 2):
            pair = held.tile([features, 2, codes], BF16, name=f"pair{first}")
            nc.scalar.dma_start(pair[:], table[first : first + 2].rearrange("f k s -> k f s"))
            windows.extend([pair[:, 0, :], pair[:, 1, :]])
        for f in range(codebooks - 2, codebooks):
            single = held.tile([features, codes], BF16, name=f"single{f}")
            nc.scalar.dma_start(single[:], table[f])
            windows.append(single[:])

        total = psum.tile([channels, frames], F32, name="total")
        for f in range(codebooks):
            picked = windows[f].indirect(offsets[:, f * list_columns : (f + 1) * list_columns])
            nc.tensor.matmul(total[:], weights[:], picked, start=(f == 0), stop=(f == codebooks - 1))

        result = held.tile([channels, frames], F32, name="result")
        nc.scalar.activation(result[:], total[:], GELU, bias=bias[:])
        nc.sync.dma_start(out, result[:])
